import numpy as np
import ml_dtypes


def mxq(x, axis, fmt="e4m3"):
    dtype, down = {"e4m3": (ml_dtypes.float8_e4m3fn, 7), "e5m2": (ml_dtypes.float8_e5m2, 14)}[fmt]
    v = np.moveaxis(np.asarray(x, np.float32).astype(ml_dtypes.bfloat16).astype(np.float64), axis, -1)
    blocks = v.reshape(v.shape[:-1] + (-1, 32))
    amax = np.abs(blocks).max(-1, keepdims=True)
    byte = np.maximum(np.where(amax > 0, np.frexp(amax)[1] - 1 + 127, 0) - down, 1)
    scale = np.exp2(byte - 127.0)
    codes = (blocks / scale).astype(np.float32).astype(dtype).astype(np.float64)
    return np.moveaxis((codes * scale).reshape(v.shape), -1, axis)


WIDE = False


def mx_kscale(k):
    if not WIDE:
        return np.ones(k)
    levels = np.array([10, -10, 5, -5, 0])
    if k % 512:
        return np.exp2(np.random.permutation(np.resize(levels, k // 32))).repeat(32)
    a = np.empty((k // 512, 16))
    for p in range(k // 512):
        a[p, :8] = np.random.permutation(np.resize(levels, 8))
        for g in range(8):
            far = levels[np.abs(levels - a[p, g]) >= 10]
            a[p, g + 8] = far[np.random.randint(len(far))]
    return np.exp2(a.ravel()).repeat(32)


def f64(x):
    return np.asarray(x).astype(np.float64)


def striped(idx):
    return np.tile(idx.reshape(-1, 16).T, (8, 1)).astype(np.uint16)


def unstriped(offs):
    return offs[:16].T.reshape(-1).astype(np.int64)


def striped8(idx):
    return np.concatenate([x.reshape(-1, 16).T for x in idx]).astype(np.uint16)


def runs(offs, k):
    lists = np.stack([offs[16 * r : 16 * r + 16].T.reshape(-1) for r in range(8)]).astype(np.int64)
    return lists[np.arange(k) % 512 // 64]


def pack_weight(w):
    k, n = w.shape
    w = f64(np.asarray(w, np.float32).astype(ml_dtypes.bfloat16)).reshape(k // 32, 32, n)
    amax = np.abs(w).max(1)
    byte = np.clip(np.where(amax > 0, np.frexp(amax)[1] - 1 + 127 - 7, 1), 1, 254)
    scaled = (w * np.exp2(127.0 - byte)[:, None, :]).reshape(k, n).astype(np.float32)
    words = np.ascontiguousarray(scaled.reshape(k // 512, 128, 4, n).transpose(0, 1, 3, 2)).astype(ml_dtypes.float8_e4m3fn).view(np.uint8)
    return words, np.ascontiguousarray(byte.astype(np.uint8).reshape(k // 512, 16, n))


def unpack_weight(words, scales):
    g, p, n, _ = words.shape
    vals = np.ascontiguousarray(words).view(ml_dtypes.float8_e4m3fn).astype(np.float64) * np.repeat(np.exp2(scales.astype(np.float64) - 127.0), 8, axis=1)[..., None]
    return vals.transpose(0, 1, 3, 2).reshape(g * 512, n)


K, T, S, N, H, W = 512, 2048, 512, 512, 512, 256


def setup_inputs():
    n = np.random.standard_normal
    s = mx_kscale(K)[:, None]
    u = mx_kscale(H)
    packed_xT = pack_weight(n((K, T)) * s)
    perm = np.random.permutation(S)
    return {
        "x_words": packed_xT[0],
        "x_scales": packed_xT[1],
        "w1": (n((K, H)) / np.sqrt(K) / s).astype(np.float32),
        "w2": (n((K, H)) / np.sqrt(K) / s).astype(np.float32),
        "gn": (np.random.uniform(0.5, 1.5, (H, 1)) * u[:, None]).astype(np.float32),
        "w3": (n((H, N)) / np.sqrt(H) / u[:, None]).astype(np.float32),
        "offs": striped(np.random.permutation(T)[:S]),
        "hz": striped8(np.random.randint(0, T, (8, S))),
        "n1": striped8(np.stack([np.random.permutation(S) for _ in range(8)])),
        "n2": striped8(np.stack([np.random.permutation(S) for _ in range(8)])),
        "n3": striped8(np.stack([np.random.permutation(S) for _ in range(8)])),
        "n4": striped8(np.stack([np.random.permutation(S) for _ in range(8)])),
        "n5": striped(perm[:W]),
        "n6": striped(perm[W:]),
    }


def reference(x_words, x_scales, w1, w2, gn, w3, offs, hz, n1, n2, n3, n4, n5, n6):
    xq = unpack_weight(x_words, x_scales)[:, unstriped(offs)]
    y = mxq(f64(w1), 0, "e4m3").T @ xq
    x_hz = unpack_weight(x_words, x_scales)[np.arange(K)[:, None], runs(hz, K)]
    d = mxq(f64(w2), 0, "e4m3").T @ x_hz
    z = f64(gn) * (np.maximum(y[np.arange(H)[:, None], runs(n1, H)] + d[np.arange(H)[:, None], runs(n3, H)], y[np.arange(H)[:, None], runs(n2, H)] + d[np.arange(H)[:, None], runs(n4, H)]))
    h = mxq(f64(w3), 0, "e4m3").T @ mxq(z, 0, "e4m3")
    pb = h[:, unstriped(n6)]
    pa = h[:, unstriped(n5)]
    rb = pb - (0.5 * pa)
    ra = np.sqrt((pa) ** 2 + (pb) ** 2 + 0.25)
    ds = np.zeros((N, S))
    ds[:, unstriped(n5)] = ra
    out = ds.copy()
    out[:, unstriped(n6)] = rb
    return out

@@ -1,0 +1,243 @@
+from contextlib import ExitStack
+
+import concourse.mybir as mybir
+
+K, T, S, N, H, W = 512, 2048, 512, 512, 512, 256
+FLOPS = 3 * 2 * 512 * 512 * 512
+
+F32 = mybir.dt.float32
+BF16 = mybir.dt.bfloat16
+U32 = mybir.dt.uint32
+I32 = mybir.dt.int32
+U16 = mybir.dt.uint16
+U8 = mybir.dt.uint8
+FP8X4 = mybir.dt.float8_e4m3fn_x4
+ALU = mybir.AluOpType
+ACT = mybir.ActivationFunctionType
+
+P = 128
+PACK = 4
+CHUNKS = ((0, 256), (256, 128), (384, 128))
+W1_VECTOR_COLUMNS = 64
+D_ON_VECTOR = 2
+FUSED_FIRST = 3
+FUSED_SECOND = 1
+H_ON_VECTOR = 2
+
+
+def tile_picked_twhpathbpolar_none_p_kernel(
+    tc, x_words, x_scales, w1, w2, gn, w3, offs, hz, n1, n2, n3, n4, n5, n6, out
+):
+    nc = tc.nc
+    with ExitStack() as ctx:
+        lists = ctx.enter_context(tc.tile_pool(name="lists", bufs=1))
+        sb = ctx.enter_context(tc.tile_pool(name="sb", bufs=1))
+        psum = ctx.enter_context(tc.psum_pool(name="psum", bufs=1))
+
+        def load_list(name, source):
+            tile = lists.tile(list(source.shape), U16, name=name)
+            nc.sync.dma_start(tile[:], source)
+            return tile
+
+        def load_weight(name, source, tag):
+            raw = sb.tile([P, PACK, H], F32, name=name, tag=tag, align_bytes=64)
+            nc.sync.dma_start(out=raw[:], in_=source.rearrange("(p j) c -> p j c", j=PACK))
+            return raw
+
+        table_scales = sb.tile([P, T], U8, name="table_scales", align_bytes=64)
+        table_scales_i = table_scales[:].bitcast(I32)
+        scale_rows = x_scales[0].bitcast(I32)
+
+        hz_t = load_list("hz_t", hz)
+        offs_t = load_list("offs_t", offs)
+        for q in range(4):
+            nc.sync.dma_start(
+                out=table_scales_i[32 * q : 32 * q + 32, :],
+                in_=scale_rows[4 * q : 4 * q + 4, :].unsqueeze(0).to_broadcast([8, 4, T // 4]),
+            )
+        w1_raw = load_weight("w1_raw", w1, "raw_a")
+        table_words = sb.tile([P, T], I32, name="table_words", align_bytes=64)
+        nc.sync.dma_start(out=table_words[:], in_=x_words[0].rearrange("p n t -> p (n t)").bitcast(I32))
+        n1_t = load_list("n1_t", n1)
+        n2_t = load_list("n2_t", n2)
+        w2_raw = load_weight("w2_raw", w2, "raw_b")
+        n3_t = load_list("n3_t", n3)
+        n4_t = load_list("n4_t", n4)
+        gain = sb.tile([P, PACK], F32, name="gain")
+        nc.sync.dma_start(out=gain[:], in_=gn.rearrange("(p t) o -> p (t o)", t=PACK))
+        n5_t = load_list("n5_t", n5)
+        n6_t = load_list("n6_t", n6)
+
+        hz_scales_raw = sb.tile([P, S], U8, name="hz_scales_raw", align_bytes=64)
+        nc.vector.tensor_copy(hz_scales_raw[:], table_scales[:].indirect(hz_t[:]))
+        tok_scales = sb.tile([P, S], U8, name="tok_scales", align_bytes=64)
+        nc.vector.tensor_copy(tok_scales[:], table_scales[:].indirect(offs_t[:]))
+        hz_scales = sb.tile([P, S], U8, name="hz_scales", align_bytes=64)
+        nc.vector.tensor_copy(hz_scales[:].bitcast(I32), hz_scales_raw[:].bitcast(I32))
+        for i in (2, 3):
+            nc.sync.dma_start(
+                out=hz_scales[:].bitcast(I32)[i:P:32, :], in_=hz_scales_raw[:].bitcast(I32)[16 + i : P : 32, :]
+            )
+
+        def deal_columns(engine_copy, grouped, raw, m0, m1):
+            engine_copy(
+                grouped[:].rearrange("p (t m j) -> p m j t", t=PACK, j=PACK)[:, m0:m1],
+                raw[:].rearrange("p j (m t) -> p m j t", t=PACK)[:, m0:m1],
+            )
+
+        def quantized_tiles(name, width):
+            codes = sb.tile([P, width], U32, name=name + "_codes", align_bytes=64)
+            scales = sb.tile([P, width], U8, name=name + "_scales", align_bytes=64)
+            return codes, scales
+
+        def quantize(codes, scales, grouped, c0, width):
+            nc.vector.quantize_mx(
+                out=codes[:, c0 : c0 + width].bitcast(FP8X4),
+                scales=scales[:, c0 : c0 + width],
+                in_=grouped[:, PACK * c0 : PACK * (c0 + width)],
+            )
+
+        def product(result, lhs, tile_index, rhs_codes, rhs_scales):
+            cols = slice(tile_index * P, (tile_index + 1) * P)
+            nc.tensor.matmul_mx(
+                out=result,
+                lhsT=lhs[0][:, cols].bitcast(FP8X4),
+                lhsT_scale=lhs[1][:, cols],
+                rhs=rhs_codes.bitcast(FP8X4),
+                rhs_scale=rhs_scales,
+                start=True,
+                stop=True,
+            )
+
+        w1_grouped = sb.tile([P, PACK * H], BF16, name="w1_grouped", align_bytes=64)
+        deal_columns(nc.vector.tensor_copy, w1_grouped, w1_raw, 0, W1_VECTOR_COLUMNS)
+        deal_columns(nc.scalar.copy, w1_grouped, w1_raw, W1_VECTOR_COLUMNS, P)
+        w3_raw = load_weight("w3_raw", w3, "raw_a")
+        w1_q = quantized_tiles("w1", H)
+        quantize(w1_q[0], w1_q[1], w1_grouped, 0, H)
+
+        tok_words = sb.tile([P, S], U32, name="tok_words", align_bytes=64)
+        nc.vector.tensor_copy(tok_words[:], table_words[:].bitcast(U32).indirect(offs_t[:]))
+        y_ps = []
+        for t in range(PACK):
+            bank = psum.tile([P, S], F32, name="y_ps%d" % t, tag="bank%d" % t)
+            product(bank[:], w1_q, t, tok_words[:], tok_scales[:])
+            y_ps.append(bank)
+
+        hz_words = sb.tile([P, S], U32, name="hz_words", align_bytes=64)
+        nc.vector.tensor_copy(hz_words[:], table_words[:].bitcast(U32).indirect(hz_t[:]))
+
+        w2_grouped = sb.tile([P, PACK * H], BF16, name="w2_grouped", align_bytes=64)
+        deal_columns(nc.vector.tensor_copy, w2_grouped, w2_raw, 0, P)
+        w2_q = quantized_tiles("w2", H)
+        d_ps = []
+        for t in range(PACK):
+            quantize(w2_q[0], w2_q[1], w2_grouped, t * P, P)
+            bank = psum.tile([P, S], F32, name="d_ps%d" % t, tag="bank%d" % (PACK + t))
+            product(bank[:], w2_q, t, hz_words[:], hz_scales[:])
+            d_ps.append(bank)
+
+        y = [sb.tile([P, S], F32, name="y%d" % t, align_bytes=64) for t in range(PACK)]
+        d = [sb.tile([P, S], F32, name="d%d" % t, align_bytes=64) for t in range(PACK)]
+        w3_grouped = sb.tile([P, PACK * N], BF16, name="w3_grouped", align_bytes=64)
+        w3_q = quantized_tiles("w3", N)
+        h_ps = []
+        h = [sb.tile([P, S], F32, name="h%d" % u, align_bytes=64) for u in range(PACK)]
+
+        def entries(list_tile, c0, width):
+            return list_tile[:, c0 // 16 : (c0 + width) // 16]
+
+        def picked_sum(name, t, y_list, d_list, c0, width, fused):
+            from_y = sb.tile([P, width], F32, name=name + "_y", align_bytes=64)
+            nc.scalar.activation(from_y[:], y[t][:].indirect(entries(y_list, c0, width)), ACT.Copy)
+            total = sb.tile([P, width], F32, name=name + "_sum", align_bytes=64)
+            if fused:
+                nc.vector.tensor_tensor(total[:], d[t][:].indirect(entries(d_list, c0, width)), from_y[:], ALU.add)
+            else:
+                from_d = sb.tile([P, width], F32, name=name + "_d", align_bytes=64)
+                nc.scalar.activation(from_d[:], d[t][:].indirect(entries(d_list, c0, width)), ACT.Copy)
+                nc.vector.tensor_tensor(total[:], from_d[:], from_y[:], ALU.add)
+            return total
+
+        for c, (c0, width) in enumerate(CHUNKS):
+            larger = sb.tile([P, PACK, width], F32, name="larger%d" % c, align_bytes=64)
+            for t in range(PACK):
+                if c == 0:
+                    nc.scalar.copy(y[t][:], y_ps[t][:])
+                    if t < D_ON_VECTOR:
+                        nc.vector.tensor_copy(d[t][:], d_ps[t][:])
+                    else:
+                        nc.scalar.copy(d[t][:], d_ps[t][:])
+                first = picked_sum("a%d_%d" % (c, t), t, n1_t, n3_t, c0, width, c < FUSED_FIRST)
+                second = picked_sum("b%d_%d" % (c, t), t, n2_t, n4_t, c0, width, c < FUSED_SECOND)
+                nc.vector.tensor_tensor(larger[:, t, :], first[:], second[:], ALU.max)
+            if c == 0:
+                nc.scalar.copy(
+                    w3_grouped[:].rearrange("p (c i j) -> p c j i", i=4, j=PACK),
+                    w3_raw[:].rearrange("p j (c i) -> p c j i", i=4),
+                )
+                quantize(w3_q[0], w3_q[1], w3_grouped, 0, N)
+                for u in range(PACK):
+                    bank = psum.tile([P, S], F32, name="h_ps%d" % u, tag="bank%d" % u)
+                    h_ps.append(bank)
+            z_grouped = sb.tile([P, PACK * width], BF16, name="z_grouped%d" % c, align_bytes=64)
+            nc.vector.tensor_tensor(
+                z_grouped[:].rearrange("p (c i t) -> p c t i", i=4, t=PACK),
+                larger[:].rearrange("p t (c i) -> p c t i", i=4),
+                gain[:].unsqueeze(1).unsqueeze(3).to_broadcast([P, width // 4, PACK, 4]),
+                ALU.mult,
+            )
+            z_q = quantized_tiles("z%d" % c, width)
+            quantize(z_q[0], z_q[1], z_grouped, 0, width)
+            for u in range(PACK):
+                product(h_ps[u][:, c0 : c0 + width], w3_q, u, z_q[0][:], z_q[1][:])
+            for u in range(PACK):
+                if c == len(CHUNKS) - 1 and u < H_ON_VECTOR:
+                    nc.vector.tensor_copy(h[u][:, c0 : c0 + width], h_ps[u][:, c0 : c0 + width])
+                else:
+                    nc.scalar.copy(h[u][:, c0 : c0 + width], h_ps[u][:, c0 : c0 + width])
+
+        pairs, squares, roots = [], [], []
+        for u in range(PACK):
+            pair = sb.tile([P, 2 * W], F32, name="pair%d" % u, align_bytes=64)
+            nc.scalar.activation(pair[:, 0:W], h[u][:].indirect(n5_t[:]), ACT.Copy, scale=-0.5)
+            nc.vector.tensor_copy(pair[:, W : 2 * W], h[u][:].indirect(n6_t[:]))
+            pairs.append(pair)
+        for u in range(PACK):
+            square = sb.tile([P, 2 * W], F32, name="square%d" % u, tag="row_tile%d" % u, align_bytes=64)
+            if u % 2 == 0:
+                nc.vector.tensor_tensor(square[:], pairs[u][:], pairs[u][:], ALU.mult)
+            else:
+                nc.scalar.activation(square[:], pairs[u][:], ACT.Square)
+            squares.append(square)
+        for u in range(PACK):
+            radicand = sb.tile([P, W], F32, name="radicand%d" % u, align_bytes=64)
+            nc.vector.scalar_tensor_tensor(
+                radicand[:], squares[u][:, 0:W], 4.0, squares[u][:, W : 2 * W], ALU.mult, ALU.add
+            )
+            ra = sb.tile([P, W], F32, name="ra%d" % u, align_bytes=64)
+            nc.scalar.activation(ra[:], radicand[:], ACT.Sqrt, bias=0.25)
+            roots.append(ra)
+        results = [
+            sb.tile([P, S], F32, name="result%d" % u, tag="row_tile%d" % (PACK - 1 - u // 2 * 2 - (1 - u % 2)), align_bytes=64)
+            for u in range(PACK)
+        ]
+
+        def put_ra(u):
+            nc.scalar.activation(results[u][:].indirect(n5_t[:]), roots[u][:], ACT.Copy)
+
+        def put_rb(u):
+            nc.vector.tensor_tensor(
+                results[u][:].indirect(n6_t[:]), pairs[u][:, W : 2 * W], pairs[u][:, 0:W], ALU.add
+            )
+
+        def store(u):
+            nc.sync.dma_start(out=out[u * P : (u + 1) * P, :], in_=results[u][:])
+
+        for u in range(0, PACK, 2):
+            put_ra(u)
+            put_rb(u + 1)
+            put_ra(u + 1)
+            put_rb(u)
+            store(u + 1)
+            store(u)

@@ -18,11 +18,11 @@ ACT = mybir.ActivationFunctionType
 P = 128
 PACK = 4
 CHUNKS = ((0, 256), (256, 128), (384, 128))
-W1_VECTOR_COLUMNS = 64
-D_ON_VECTOR = 2
-FUSED_FIRST = 3
-FUSED_SECOND = 1
+D_ON_VECTOR = 4
+FUSED_FIRST = (0, 1)
+FUSED_SECOND = (0, 1)
 H_ON_VECTOR = 2
+SQUARES_ON_VECTOR = ()
 
 
 def tile_picked_twhpathbpolar_none_p_kernel(
@@ -32,6 +32,7 @@ def tile_picked_twhpathbpolar_none_p_kernel(
     with ExitStack() as ctx:
         lists = ctx.enter_context(tc.tile_pool(name="lists", bufs=1))
         sb = ctx.enter_context(tc.tile_pool(name="sb", bufs=1))
+        shared = ctx.enter_context(tc.tile_pool(name="shared", bufs=1))
         psum = ctx.enter_context(tc.psum_pool(name="psum", bufs=1))
 
         def load_list(name, source):
@@ -63,10 +64,6 @@ def tile_picked_twhpathbpolar_none_p_kernel(
         w2_raw = load_weight("w2_raw", w2, "raw_b")
         n3_t = load_list("n3_t", n3)
         n4_t = load_list("n4_t", n4)
-        gain = sb.tile([P, PACK], F32, name="gain")
-        nc.sync.dma_start(out=gain[:], in_=gn.rearrange("(p t) o -> p (t o)", t=PACK))
-        n5_t = load_list("n5_t", n5)
-        n6_t = load_list("n6_t", n6)
 
         hz_scales_raw = sb.tile([P, S], U8, name="hz_scales_raw", align_bytes=64)
         nc.vector.tensor_copy(hz_scales_raw[:], table_scales[:].indirect(hz_t[:]))
@@ -75,14 +72,18 @@ def tile_picked_twhpathbpolar_none_p_kernel(
         hz_scales = sb.tile([P, S], U8, name="hz_scales", align_bytes=64)
         nc.vector.tensor_copy(hz_scales[:].bitcast(I32), hz_scales_raw[:].bitcast(I32))
         for i in (2, 3):
-            nc.sync.dma_start(
+            nc.gpsimd.dma_start(
                 out=hz_scales[:].bitcast(I32)[i:P:32, :], in_=hz_scales_raw[:].bitcast(I32)[16 + i : P : 32, :]
             )
+        gain = sb.tile([P, PACK], F32, name="gain")
+        nc.gpsimd.dma_start(out=gain[:], in_=gn.rearrange("(p t) o -> p (t o)", t=PACK))
+        n5_t = load_list("n5_t", n5)
+        n6_t = load_list("n6_t", n6)
 
-        def deal_columns(engine_copy, grouped, raw, m0, m1):
+        def deal_columns(engine_copy, grouped, raw, t0, t1):
             engine_copy(
-                grouped[:].rearrange("p (t m j) -> p m j t", t=PACK, j=PACK)[:, m0:m1],
-                raw[:].rearrange("p j (m t) -> p m j t", t=PACK)[:, m0:m1],
+                grouped[:].rearrange("p (t m j) -> p m j t", t=t1 - t0, j=PACK),
+                raw[:].rearrange("p j (m t) -> p m j t", t=PACK)[:, :, :, t0:t1],
             )
 
         def quantized_tiles(name, width):
@@ -109,37 +110,39 @@ def tile_picked_twhpathbpolar_none_p_kernel(
                 stop=True,
             )
 
-        w1_grouped = sb.tile([P, PACK * H], BF16, name="w1_grouped", align_bytes=64)
-        deal_columns(nc.vector.tensor_copy, w1_grouped, w1_raw, 0, W1_VECTOR_COLUMNS)
-        deal_columns(nc.scalar.copy, w1_grouped, w1_raw, W1_VECTOR_COLUMNS, P)
-        w3_raw = load_weight("w3_raw", w3, "raw_a")
-        w1_q = quantized_tiles("w1", H)
-        quantize(w1_q[0], w1_q[1], w1_grouped, 0, H)
+        w1_q = []
+        for half, engine_copy in enumerate((nc.vector.tensor_copy, nc.scalar.copy)):
+            grouped = sb.tile([P, PACK * H // 2], BF16, name="w1_grouped%d" % half, align_bytes=64)
+            deal_columns(engine_copy, grouped, w1_raw, 2 * half, 2 * half + 2)
+            half_q = quantized_tiles("w1_%d" % half, H // 2)
+            quantize(half_q[0], half_q[1], grouped, 0, H // 2)
+            w1_q.append(half_q)
 
         tok_words = sb.tile([P, S], U32, name="tok_words", align_bytes=64)
         nc.vector.tensor_copy(tok_words[:], table_words[:].bitcast(U32).indirect(offs_t[:]))
         y_ps = []
         for t in range(PACK):
             bank = psum.tile([P, S], F32, name="y_ps%d" % t, tag="bank%d" % t)
-            product(bank[:], w1_q, t, tok_words[:], tok_scales[:])
+            product(bank[:], w1_q[t // 2], t % 2, tok_words[:], tok_scales[:])
             y_ps.append(bank)
 
-        hz_words = sb.tile([P, S], U32, name="hz_words", align_bytes=64)
+        hz_words = sb.tile([P, S], U32, name="hz_words", tag="late", align_bytes=64)
         nc.vector.tensor_copy(hz_words[:], table_words[:].bitcast(U32).indirect(hz_t[:]))
 
-        w2_grouped = sb.tile([P, PACK * H], BF16, name="w2_grouped", align_bytes=64)
-        deal_columns(nc.vector.tensor_copy, w2_grouped, w2_raw, 0, P)
-        w2_q = quantized_tiles("w2", H)
         d_ps = []
-        for t in range(PACK):
-            quantize(w2_q[0], w2_q[1], w2_grouped, t * P, P)
-            bank = psum.tile([P, S], F32, name="d_ps%d" % t, tag="bank%d" % (PACK + t))
-            product(bank[:], w2_q, t, hz_words[:], hz_scales[:])
-            d_ps.append(bank)
+        for half in range(2):
+            grouped = sb.tile([P, PACK * H // 2], BF16, name="w2_grouped%d" % half, align_bytes=64)
+            deal_columns(nc.vector.tensor_copy, grouped, w2_raw, 2 * half, 2 * half + 2)
+            half_q = quantized_tiles("w2_%d" % half, H // 2)
+            quantize(half_q[0], half_q[1], grouped, 0, H // 2)
+            for t in range(2):
+                bank = psum.tile([P, S], F32, name="d_ps%d" % (2 * half + t), tag="bank%d" % (PACK + 2 * half + t))
+                product(bank[:], half_q, t, hz_words[:], hz_scales[:])
+                d_ps.append(bank)
 
+        w3_raw = load_weight("w3_raw", w3, "raw_b")
         y = [sb.tile([P, S], F32, name="y%d" % t, align_bytes=64) for t in range(PACK)]
         d = [sb.tile([P, S], F32, name="d%d" % t, align_bytes=64) for t in range(PACK)]
-        w3_grouped = sb.tile([P, PACK * N], BF16, name="w3_grouped", align_bytes=64)
         w3_q = quantized_tiles("w3", N)
         h_ps = []
         h = [sb.tile([P, S], F32, name="h%d" % u, align_bytes=64) for u in range(PACK)]
@@ -147,31 +150,54 @@ def tile_picked_twhpathbpolar_none_p_kernel(
         def entries(list_tile, c0, width):
             return list_tile[:, c0 // 16 : (c0 + width) // 16]
 
-        def picked_sum(name, t, y_list, d_list, c0, width, fused):
-            from_y = sb.tile([P, width], F32, name=name + "_y", align_bytes=64)
-            nc.scalar.activation(from_y[:], y[t][:].indirect(entries(y_list, c0, width)), ACT.Copy)
-            total = sb.tile([P, width], F32, name=name + "_sum", align_bytes=64)
+        gain_size = sb.tile([P, PACK], F32, name="gain_size")
+        nc.scalar.activation(gain_size[:], gain[:], ACT.Abs)
+        gain_sign = sb.tile([P, PACK], F32, name="gain_sign")
+        nc.vector.tensor_scalar(gain_sign[:], gain[:], 0.0, 2.0, ALU.is_ge, ALU.mult)
+        signs = sb.tile([P, CHUNKS[0][1], PACK], BF16, name="signs", align_bytes=64)
+        nc.vector.tensor_scalar(
+            signs[:], gain_sign[:].unsqueeze(1).to_broadcast([P, CHUNKS[0][1], PACK]), -1.0, None, ALU.add
+        )
+
+        def branch_sums(name, c, y_list, d_list, fused, before_tile):
+            c0, width = CHUNKS[c]
+            total = sb.tile([P, PACK, width], F32, name="%s_sum%d" % (name, c), align_bytes=64)
             if fused:
-                nc.vector.tensor_tensor(total[:], d[t][:].indirect(entries(d_list, c0, width)), from_y[:], ALU.add)
+                from_y = [
+                    sb.tile([P, width], F32, name="%s_y%d_%d" % (name, c, t), tag="%s_y%d" % (name, t), align_bytes=64)[:]
+                    for t in range(PACK)
+                ]
             else:
-                from_d = sb.tile([P, width], F32, name=name + "_d", align_bytes=64)
-                nc.scalar.activation(from_d[:], d[t][:].indirect(entries(d_list, c0, width)), ACT.Copy)
-                nc.vector.tensor_tensor(total[:], from_d[:], from_y[:], ALU.add)
-            return total
+                all_y = sb.tile([P, PACK, width], F32, name="%s_y%d" % (name, c), tag="%s_y%d" % (name, c), align_bytes=64)
+                all_d = sb.tile([P, PACK, width], F32, name="%s_d%d" % (name, c), align_bytes=64)
+                from_y = [all_y[:, t, :] for t in range(PACK)]
+
+            def step(t):
+                nc.scalar.activation(from_y[t], y[t][:].indirect(entries(y_list, c0, width)), ACT.Copy)
+                picked_d = d[t][:].indirect(entries(d_list, c0, width))
+                if fused:
+                    nc.vector.tensor_tensor(total[:, t, :], picked_d, from_y[t], ALU.add)
+                else:
+                    nc.scalar.activation(all_d[:, t, :], picked_d, ACT.Copy)
+                    if t == PACK - 1:
+                        nc.vector.tensor_tensor(total[:], all_d[:], all_y[:], ALU.add)
+
+            return total, step
 
         for c, (c0, width) in enumerate(CHUNKS):
-            larger = sb.tile([P, PACK, width], F32, name="larger%d" % c, align_bytes=64)
+            first, first_step = branch_sums("first", c, n1_t, n3_t, c in FUSED_FIRST, None)
+            second, second_step = branch_sums("second", c, n2_t, n4_t, c in FUSED_SECOND, None)
             for t in range(PACK):
                 if c == 0:
-                    nc.scalar.copy(y[t][:], y_ps[t][:])
+                    nc.scalar.activation(y[t][:], y_ps[t][:], ACT.Copy, scale=gain_size[:, t : t + 1])
                     if t < D_ON_VECTOR:
-                        nc.vector.tensor_copy(d[t][:], d_ps[t][:])
+                        nc.vector.tensor_scalar(d[t][:], d_ps[t][:], gain_size[:, t : t + 1], None, ALU.mult)
                     else:
-                        nc.scalar.copy(d[t][:], d_ps[t][:])
-                first = picked_sum("a%d_%d" % (c, t), t, n1_t, n3_t, c0, width, c < FUSED_FIRST)
-                second = picked_sum("b%d_%d" % (c, t), t, n2_t, n4_t, c0, width, c < FUSED_SECOND)
-                nc.vector.tensor_tensor(larger[:, t, :], first[:], second[:], ALU.max)
+                        nc.scalar.activation(d[t][:], d_ps[t][:], ACT.Copy, scale=gain_size[:, t : t + 1])
+                first_step(t)
+                second_step(t)
             if c == 0:
+                w3_grouped = sb.tile([P, PACK * N], BF16, name="w3_grouped", tag="late", align_bytes=64)
                 nc.scalar.copy(
                     w3_grouped[:].rearrange("p (c i j) -> p c j i", i=4, j=PACK),
                     w3_raw[:].rearrange("p j (c i) -> p c j i", i=4),
@@ -180,12 +206,16 @@ def tile_picked_twhpathbpolar_none_p_kernel(
                 for u in range(PACK):
                     bank = psum.tile([P, S], F32, name="h_ps%d" % u, tag="bank%d" % u)
                     h_ps.append(bank)
+            z_size = sb.tile([P, PACK * width], BF16, name="z_size%d" % c, align_bytes=64)
+            nc.vector.tensor_tensor(
+                z_size[:].rearrange("p (c i t) -> p c t i", i=4, t=PACK),
+                first[:].rearrange("p t (c i) -> p c t i", i=4),
+                second[:].rearrange("p t (c i) -> p c t i", i=4),
+                ALU.max,
+            )
             z_grouped = sb.tile([P, PACK * width], BF16, name="z_grouped%d" % c, align_bytes=64)
             nc.vector.tensor_tensor(
-                z_grouped[:].rearrange("p (c i t) -> p c t i", i=4, t=PACK),
-                larger[:].rearrange("p t (c i) -> p c t i", i=4),
-                gain[:].unsqueeze(1).unsqueeze(3).to_broadcast([P, width // 4, PACK, 4]),
-                ALU.mult,
+                z_grouped[:], z_size[:], signs[:, 0:width, :].rearrange("p s t -> p (s t)"), ALU.mult
             )
             z_q = quantized_tiles("z%d" % c, width)
             quantize(z_q[0], z_q[1], z_grouped, 0, width)
@@ -197,47 +227,40 @@ def tile_picked_twhpathbpolar_none_p_kernel(
                 else:
                     nc.scalar.copy(h[u][:, c0 : c0 + width], h_ps[u][:, c0 : c0 + width])
 
-        pairs, squares, roots = [], [], []
+        pairs, roots = [], []
         for u in range(PACK):
             pair = sb.tile([P, 2 * W], F32, name="pair%d" % u, align_bytes=64)
             nc.scalar.activation(pair[:, 0:W], h[u][:].indirect(n5_t[:]), ACT.Copy, scale=-0.5)
             nc.vector.tensor_copy(pair[:, W : 2 * W], h[u][:].indirect(n6_t[:]))
             pairs.append(pair)
-        for u in range(PACK):
-            square = sb.tile([P, 2 * W], F32, name="square%d" % u, tag="row_tile%d" % u, align_bytes=64)
-            if u % 2 == 0:
-                nc.vector.tensor_tensor(square[:], pairs[u][:], pairs[u][:], ALU.mult)
-            else:
-                nc.scalar.activation(square[:], pairs[u][:], ACT.Square)
-            squares.append(square)
-        for u in range(PACK):
-            radicand = sb.tile([P, W], F32, name="radicand%d" % u, align_bytes=64)
-            nc.vector.scalar_tensor_tensor(
-                radicand[:], squares[u][:, 0:W], 4.0, squares[u][:, W : 2 * W], ALU.mult, ALU.add
-            )
-            ra = sb.tile([P, W], F32, name="ra%d" % u, align_bytes=64)
-            nc.scalar.activation(ra[:], radicand[:], ACT.Sqrt, bias=0.25)
-            roots.append(ra)
-        results = [
-            sb.tile([P, S], F32, name="result%d" % u, tag="row_tile%d" % (PACK - 1 - u // 2 * 2 - (1 - u % 2)), align_bytes=64)
-            for u in range(PACK)
-        ]
-
-        def put_ra(u):
-            nc.scalar.activation(results[u][:].indirect(n5_t[:]), roots[u][:], ACT.Copy)
+        squares = shared.tile([P, PACK, 2 * W], F32, name="squares", offset=0)
+        results = [sb.tile([P, S], F32, name="result0", align_bytes=64)]
 
         def put_rb(u):
             nc.vector.tensor_tensor(
                 results[u][:].indirect(n6_t[:]), pairs[u][:, W : 2 * W], pairs[u][:, 0:W], ALU.add
             )
 
-        def store(u):
-            nc.sync.dma_start(out=out[u * P : (u + 1) * P, :], in_=results[u][:])
-
-        for u in range(0, PACK, 2):
-            put_ra(u)
-            put_rb(u + 1)
-            put_ra(u + 1)
+        for u in range(PACK):
+            if u in SQUARES_ON_VECTOR:
+                nc.vector.tensor_tensor(squares[:, u, :], pairs[u][:], pairs[u][:], ALU.mult)
+            else:
+                nc.scalar.activation(squares[:, u, :], pairs[u][:], ACT.Square)
+        put_rb(0)
+        for u in range(PACK):
+            radicand = sb.tile([P, W], F32, name="radicand%d" % u, align_bytes=64)
+            nc.vector.scalar_tensor_tensor(
+                radicand[:], squares[:, u, 0:W], 4.0, squares[:, u, W : 2 * W], ALU.mult, ALU.add
+            )
+            ra = sb.tile([P, W], F32, name="ra%d" % u, align_bytes=64)
+            nc.scalar.activation(ra[:], radicand[:], ACT.Sqrt, bias=0.25)
+            roots.append(ra)
+        for u in range(1, PACK):
+            results.append(shared.tile([P, S], F32, name="result%d" % u, offset=u * S * 4))
             put_rb(u)
-            store(u + 1)
-            store(u)
+        for u in range(PACK):
+            if u < PACK - 1:
+                nc.scalar.activation(results[u][:].indirect(n5_t[:]), roots[u][:], ACT.Copy)
+            else:
+                nc.vector.tensor_copy(results[u][:].indirect(n5_t[:]), roots[u][:])
+            nc.sync.dma_start(out=out[u * P : (u + 1) * P, :], in_=results[u][:])

@@ -19,10 +19,10 @@ P = 128
 PACK = 4
 CHUNKS = ((0, 256), (256, 128), (384, 128))
 D_ON_VECTOR = 4
-FUSED_FIRST = (0, 1)
-FUSED_SECOND = (0, 1)
+FUSED_FIRST = (0, 2)
+FUSED_SECOND = (0,)
 H_ON_VECTOR = 2
-SQUARES_ON_VECTOR = ()
+GATE = 1
 
 
 def tile_picked_twhpathbpolar_none_p_kernel(
@@ -32,7 +32,6 @@ def tile_picked_twhpathbpolar_none_p_kernel(
     with ExitStack() as ctx:
         lists = ctx.enter_context(tc.tile_pool(name="lists", bufs=1))
         sb = ctx.enter_context(tc.tile_pool(name="sb", bufs=1))
-        shared = ctx.enter_context(tc.tile_pool(name="shared", bufs=1))
         psum = ctx.enter_context(tc.psum_pool(name="psum", bufs=1))
 
         def load_list(name, source):
@@ -49,6 +48,9 @@ def tile_picked_twhpathbpolar_none_p_kernel(
         table_scales_i = table_scales[:].bitcast(I32)
         scale_rows = x_scales[0].bitcast(I32)
 
+        warm = sb.tile([P, 1], F32, name="warm")
+        nc.gpsimd.memset(warm[:], 1.0)
+        nc.scalar.activation(warm[:], warm[:], ACT.Sqrt)
         hz_t = load_list("hz_t", hz)
         offs_t = load_list("offs_t", offs)
         for q in range(4):
@@ -59,6 +61,8 @@ def tile_picked_twhpathbpolar_none_p_kernel(
         w1_raw = load_weight("w1_raw", w1, "raw_a")
         table_words = sb.tile([P, T], I32, name="table_words", align_bytes=64)
         nc.sync.dma_start(out=table_words[:], in_=x_words[0].rearrange("p n t -> p (n t)").bitcast(I32))
+        gain = sb.tile([P, PACK], F32, name="gain")
+        nc.sync.dma_start(out=gain[:], in_=gn.rearrange("(p t) o -> p (t o)", t=PACK))
         n1_t = load_list("n1_t", n1)
         n2_t = load_list("n2_t", n2)
         w2_raw = load_weight("w2_raw", w2, "raw_b")
@@ -72,11 +76,9 @@ def tile_picked_twhpathbpolar_none_p_kernel(
         hz_scales = sb.tile([P, S], U8, name="hz_scales", align_bytes=64)
         nc.vector.tensor_copy(hz_scales[:].bitcast(I32), hz_scales_raw[:].bitcast(I32))
         for i in (2, 3):
-            nc.gpsimd.dma_start(
+            nc.sync.dma_start(
                 out=hz_scales[:].bitcast(I32)[i:P:32, :], in_=hz_scales_raw[:].bitcast(I32)[16 + i : P : 32, :]
             )
-        gain = sb.tile([P, PACK], F32, name="gain")
-        nc.gpsimd.dma_start(out=gain[:], in_=gn.rearrange("(p t) o -> p (t o)", t=PACK))
         n5_t = load_list("n5_t", n5)
         n6_t = load_list("n6_t", n6)
 
@@ -152,25 +154,22 @@ def tile_picked_twhpathbpolar_none_p_kernel(
 
         gain_size = sb.tile([P, PACK], F32, name="gain_size")
         nc.scalar.activation(gain_size[:], gain[:], ACT.Abs)
-        gain_sign = sb.tile([P, PACK], F32, name="gain_sign")
-        nc.vector.tensor_scalar(gain_sign[:], gain[:], 0.0, 2.0, ALU.is_ge, ALU.mult)
         signs = sb.tile([P, CHUNKS[0][1], PACK], BF16, name="signs", align_bytes=64)
-        nc.vector.tensor_scalar(
-            signs[:], gain_sign[:].unsqueeze(1).to_broadcast([P, CHUNKS[0][1], PACK]), -1.0, None, ALU.add
-        )
+        nc.scalar.activation(signs[:], gain[:].unsqueeze(1).to_broadcast([P, CHUNKS[0][1], PACK]), ACT.Sign)
 
         def branch_sums(name, c, y_list, d_list, fused, before_tile):
             c0, width = CHUNKS[c]
             total = sb.tile([P, PACK, width], F32, name="%s_sum%d" % (name, c), align_bytes=64)
-            if fused:
+            if c == 0:
                 from_y = [
-                    sb.tile([P, width], F32, name="%s_y%d_%d" % (name, c, t), tag="%s_y%d" % (name, t), align_bytes=64)[:]
+                    sb.tile([P, width], F32, name="%s_y0_%d" % (name, t), tag="%s_y%d" % (name, t), align_bytes=64)[:]
                     for t in range(PACK)
                 ]
             else:
-                all_y = sb.tile([P, PACK, width], F32, name="%s_y%d" % (name, c), tag="%s_y%d" % (name, c), align_bytes=64)
-                all_d = sb.tile([P, PACK, width], F32, name="%s_d%d" % (name, c), align_bytes=64)
+                all_y = sb.tile([P, PACK, width], F32, name="%s_y%d" % (name, c), tag="%s_y%d" % (name, c - 1 + GATE), align_bytes=64)
                 from_y = [all_y[:, t, :] for t in range(PACK)]
+            if not fused:
+                all_d = sb.tile([P, PACK, width], F32, name="%s_d%d" % (name, c), align_bytes=64)
 
             def step(t):
                 nc.scalar.activation(from_y[t], y[t][:].indirect(entries(y_list, c0, width)), ACT.Copy)
@@ -198,7 +197,7 @@ def tile_picked_twhpathbpolar_none_p_kernel(
                 second_step(t)
             if c == 0:
                 w3_grouped = sb.tile([P, PACK * N], BF16, name="w3_grouped", tag="late", align_bytes=64)
-                nc.scalar.copy(
+                nc.vector.tensor_copy(
                     w3_grouped[:].rearrange("p (c i j) -> p c j i", i=4, j=PACK),
                     w3_raw[:].rearrange("p j (c i) -> p c j i", i=4),
                 )
@@ -227,40 +226,49 @@ def tile_picked_twhpathbpolar_none_p_kernel(
                 else:
                     nc.scalar.copy(h[u][:, c0 : c0 + width], h_ps[u][:, c0 : c0 + width])
 
-        pairs, roots = [], []
+        pairs, squares, roots = [], [], []
         for u in range(PACK):
             pair = sb.tile([P, 2 * W], F32, name="pair%d" % u, align_bytes=64)
             nc.scalar.activation(pair[:, 0:W], h[u][:].indirect(n5_t[:]), ACT.Copy, scale=-0.5)
             nc.vector.tensor_copy(pair[:, W : 2 * W], h[u][:].indirect(n6_t[:]))
             pairs.append(pair)
-        squares = shared.tile([P, PACK, 2 * W], F32, name="squares", offset=0)
-        results = [sb.tile([P, S], F32, name="result0", align_bytes=64)]
+        for u in range(PACK):
+            square = sb.tile([P, 2 * W], F32, name="square%d" % u, tag="row_tile%d" % u, align_bytes=64)
+            if u % 2 == 0:
+                nc.vector.tensor_tensor(square[:], pairs[u][:], pairs[u][:], ALU.mult)
+            else:
+                nc.scalar.activation(square[:], pairs[u][:], ACT.Square)
+            squares.append(square)
+        for u in range(PACK):
+            radicand = sb.tile([P, W], F32, name="radicand%d" % u, align_bytes=64)
+            nc.vector.scalar_tensor_tensor(
+                radicand[:], squares[u][:, 0:W], 4.0, squares[u][:, W : 2 * W], ALU.mult, ALU.add
+            )
+            ra = sb.tile([P, W], F32, name="ra%d" % u, align_bytes=64)
+            nc.scalar.activation(ra[:], radicand[:], ACT.Sqrt, bias=0.25)
+            roots.append(ra)
+        results = [
+            sb.tile([P, S], F32, name="result%d" % u, tag="row_tile%d" % (0, 2, 1, 3)[u], align_bytes=64)
+            for u in range(PACK)
+        ]
+
+        def put_ra(u):
+            nc.scalar.activation(results[u][:].indirect(n5_t[:]), roots[u][:], ACT.Copy)
 
         def put_rb(u):
             nc.vector.tensor_tensor(
                 results[u][:].indirect(n6_t[:]), pairs[u][:, W : 2 * W], pairs[u][:, 0:W], ALU.add
             )
 
-        for u in range(PACK):
-            if u in SQUARES_ON_VECTOR:
-                nc.vector.tensor_tensor(squares[:, u, :], pairs[u][:], pairs[u][:], ALU.mult)
-            else:
-                nc.scalar.activation(squares[:, u, :], pairs[u][:], ACT.Square)
-        put_rb(0)
-        for u in range(PACK):
-            radicand = sb.tile([P, W], F32, name="radicand%d" % u, align_bytes=64)
-            nc.vector.scalar_tensor_tensor(
-                radicand[:], squares[:, u, 0:W], 4.0, squares[:, u, W : 2 * W], ALU.mult, ALU.add
-            )
-            ra = sb.tile([P, W], F32, name="ra%d" % u, align_bytes=64)
-            nc.scalar.activation(ra[:], radicand[:], ACT.Sqrt, bias=0.25)
-            roots.append(ra)
-        for u in range(1, PACK):
-            results.append(shared.tile([P, S], F32, name="result%d" % u, offset=u * S * 4))
+        def store(u):
+            queue = nc.scalar if u % 2 == 0 else nc.sync
+            queue.dma_start(out=out[u * P : (u + 1) * P, :], in_=results[u][:])
+
+        for u in range(0, PACK, 2):
+            put_ra(u)
+            put_rb(u + 1)
+        for u in range(0, PACK, 2):
             put_rb(u)
-        for u in range(PACK):
-            if u < PACK - 1:
-                nc.scalar.activation(results[u][:].indirect(n5_t[:]), roots[u][:], ACT.Copy)
-            else:
-                nc.vector.tensor_copy(results[u][:].indirect(n5_t[:]), roots[u][:])
-            nc.sync.dma_start(out=out[u * P : (u + 1) * P, :], in_=results[u][:])
+            store(u)
+            put_ra(u + 1)
+            store(u + 1)

from contextlib import ExitStack

import concourse.mybir as mybir

K, T, S, N, H, W = 512, 2048, 512, 512, 512, 256
FLOPS = 3 * 2 * 512 * 512 * 512

F32 = mybir.dt.float32
BF16 = mybir.dt.bfloat16
U32 = mybir.dt.uint32
I32 = mybir.dt.int32
U16 = mybir.dt.uint16
U8 = mybir.dt.uint8
FP8X4 = mybir.dt.float8_e4m3fn_x4
ALU = mybir.AluOpType
ACT = mybir.ActivationFunctionType

P = 128
PACK = 4
CHUNKS = ((0, 256), (256, 128), (384, 128))
D_ON_VECTOR = 4
FUSED_FIRST = (0, 2)
FUSED_SECOND = (0,)
H_ON_VECTOR = 2
GATE = 1


def tile_picked_twhpathbpolar_none_p_kernel(
    tc, x_words, x_scales, w1, w2, gn, w3, offs, hz, n1, n2, n3, n4, n5, n6, out
):
    nc = tc.nc
    with ExitStack() as ctx:
        lists = ctx.enter_context(tc.tile_pool(name="lists", bufs=1))
        sb = ctx.enter_context(tc.tile_pool(name="sb", bufs=1))
        psum = ctx.enter_context(tc.psum_pool(name="psum", bufs=1))

        def load_list(name, source):
            tile = lists.tile(list(source.shape), U16, name=name)
            nc.sync.dma_start(tile[:], source)
            return tile

        def load_weight(name, source, tag):
            raw = sb.tile([P, PACK, H], F32, name=name, tag=tag, align_bytes=64)
            nc.sync.dma_start(out=raw[:], in_=source.rearrange("(p j) c -> p j c", j=PACK))
            return raw

        table_scales = sb.tile([P, T], U8, name="table_scales", align_bytes=64)
        table_scales_i = table_scales[:].bitcast(I32)
        scale_rows = x_scales[0].bitcast(I32)

        warm = sb.tile([P, 1], F32, name="warm")
        nc.gpsimd.memset(warm[:], 1.0)
        nc.scalar.activation(warm[:], warm[:], ACT.Sqrt)
        hz_t = load_list("hz_t", hz)
        offs_t = load_list("offs_t", offs)
        for q in range(4):
            nc.sync.dma_start(
                out=table_scales_i[32 * q : 32 * q + 32, :],
                in_=scale_rows[4 * q : 4 * q + 4, :].unsqueeze(0).to_broadcast([8, 4, T // 4]),
            )
        w1_raw = load_weight("w1_raw", w1, "raw_a")
        table_words = sb.tile([P, T], I32, name="table_words", align_bytes=64)
        nc.sync.dma_start(out=table_words[:], in_=x_words[0].rearrange("p n t -> p (n t)").bitcast(I32))
        gain = sb.tile([P, PACK], F32, name="gain")
        nc.sync.dma_start(out=gain[:], in_=gn.rearrange("(p t) o -> p (t o)", t=PACK))
        n1_t = load_list("n1_t", n1)
        n2_t = load_list("n2_t", n2)
        w2_raw = load_weight("w2_raw", w2, "raw_b")
        n3_t = load_list("n3_t", n3)
        n4_t = load_list("n4_t", n4)

        hz_scales_raw = sb.tile([P, S], U8, name="hz_scales_raw", align_bytes=64)
        nc.vector.tensor_copy(hz_scales_raw[:], table_scales[:].indirect(hz_t[:]))
        tok_scales = sb.tile([P, S], U8, name="tok_scales", align_bytes=64)
        nc.vector.tensor_copy(tok_scales[:], table_scales[:].indirect(offs_t[:]))
        hz_scales = sb.tile([P, S], U8, name="hz_scales", align_bytes=64)
        nc.vector.tensor_copy(hz_scales[:].bitcast(I32), hz_scales_raw[:].bitcast(I32))
        for i in (2, 3):
            nc.sync.dma_start(
                out=hz_scales[:].bitcast(I32)[i:P:32, :], in_=hz_scales_raw[:].bitcast(I32)[16 + i : P : 32, :]
            )
        n5_t = load_list("n5_t", n5)
        n6_t = load_list("n6_t", n6)

        def deal_columns(engine_copy, grouped, raw, t0, t1):
            engine_copy(
                grouped[:].rearrange("p (t m j) -> p m j t", t=t1 - t0, j=PACK),
                raw[:].rearrange("p j (m t) -> p m j t", t=PACK)[:, :, :, t0:t1],
            )

        def quantized_tiles(name, width):
            codes = sb.tile([P, width], U32, name=name + "_codes", align_bytes=64)
            scales = sb.tile([P, width], U8, name=name + "_scales", align_bytes=64)
            return codes, scales

        def quantize(codes, scales, grouped, c0, width):
            nc.vector.quantize_mx(
                out=codes[:, c0 : c0 + width].bitcast(FP8X4),
                scales=scales[:, c0 : c0 + width],
                in_=grouped[:, PACK * c0 : PACK * (c0 + width)],
            )

        def product(result, lhs, tile_index, rhs_codes, rhs_scales):
            cols = slice(tile_index * P, (tile_index + 1) * P)
            nc.tensor.matmul_mx(
                out=result,
                lhsT=lhs[0][:, cols].bitcast(FP8X4),
                lhsT_scale=lhs[1][:, cols],
                rhs=rhs_codes.bitcast(FP8X4),
                rhs_scale=rhs_scales,
                start=True,
                stop=True,
            )

        w1_q = []
        for half, engine_copy in enumerate((nc.vector.tensor_copy, nc.scalar.copy)):
            grouped = sb.tile([P, PACK * H // 2], BF16, name="w1_grouped%d" % half, align_bytes=64)
            deal_columns(engine_copy, grouped, w1_raw, 2 * half, 2 * half + 2)
            half_q = quantized_tiles("w1_%d" % half, H // 2)
            quantize(half_q[0], half_q[1], grouped, 0, H // 2)
            w1_q.append(half_q)

        tok_words = sb.tile([P, S], U32, name="tok_words", align_bytes=64)
        nc.vector.tensor_copy(tok_words[:], table_words[:].bitcast(U32).indirect(offs_t[:]))
        y_ps = []
        for t in range(PACK):
            bank = psum.tile([P, S], F32, name="y_ps%d" % t, tag="bank%d" % t)
            product(bank[:], w1_q[t // 2], t % 2, tok_words[:], tok_scales[:])
            y_ps.append(bank)

        hz_words = sb.tile([P, S], U32, name="hz_words", tag="late", align_bytes=64)
        nc.vector.tensor_copy(hz_words[:], table_words[:].bitcast(U32).indirect(hz_t[:]))

        d_ps = []
        for half in range(2):
            grouped = sb.tile([P, PACK * H // 2], BF16, name="w2_grouped%d" % half, align_bytes=64)
            deal_columns(nc.vector.tensor_copy, grouped, w2_raw, 2 * half, 2 * half + 2)
            half_q = quantized_tiles("w2_%d" % half, H // 2)
            quantize(half_q[0], half_q[1], grouped, 0, H // 2)
            for t in range(2):
                bank = psum.tile([P, S], F32, name="d_ps%d" % (2 * half + t), tag="bank%d" % (PACK + 2 * half + t))
                product(bank[:], half_q, t, hz_words[:], hz_scales[:])
                d_ps.append(bank)

        w3_raw = load_weight("w3_raw", w3, "raw_b")
        y = [sb.tile([P, S], F32, name="y%d" % t, align_bytes=64) for t in range(PACK)]
        d = [sb.tile([P, S], F32, name="d%d" % t, align_bytes=64) for t in range(PACK)]
        w3_q = quantized_tiles("w3", N)
        h_ps = []
        h = [sb.tile([P, S], F32, name="h%d" % u, align_bytes=64) for u in range(PACK)]

        def entries(list_tile, c0, width):
            return list_tile[:, c0 // 16 : (c0 + width) // 16]

        gain_size = sb.tile([P, PACK], F32, name="gain_size")
        nc.scalar.activation(gain_size[:], gain[:], ACT.Abs)
        signs = sb.tile([P, CHUNKS[0][1], PACK], BF16, name="signs", align_bytes=64)
        nc.scalar.activation(signs[:], gain[:].unsqueeze(1).to_broadcast([P, CHUNKS[0][1], PACK]), ACT.Sign)

        def branch_sums(name, c, y_list, d_list, fused, before_tile):
            c0, width = CHUNKS[c]
            total = sb.tile([P, PACK, width], F32, name="%s_sum%d" % (name, c), align_bytes=64)
            if c == 0:
                from_y = [
                    sb.tile([P, width], F32, name="%s_y0_%d" % (name, t), tag="%s_y%d" % (name, t), align_bytes=64)[:]
                    for t in range(PACK)
                ]
            else:
                all_y = sb.tile([P, PACK, width], F32, name="%s_y%d" % (name, c), tag="%s_y%d" % (name, c - 1 + GATE), align_bytes=64)
                from_y = [all_y[:, t, :] for t in range(PACK)]
            if not fused:
                all_d = sb.tile([P, PACK, width], F32, name="%s_d%d" % (name, c), align_bytes=64)

            def step(t):
                nc.scalar.activation(from_y[t], y[t][:].indirect(entries(y_list, c0, width)), ACT.Copy)
                picked_d = d[t][:].indirect(entries(d_list, c0, width))
                if fused:
                    nc.vector.tensor_tensor(total[:, t, :], picked_d, from_y[t], ALU.add)
                else:
                    nc.scalar.activation(all_d[:, t, :], picked_d, ACT.Copy)
                    if t == PACK - 1:
                        nc.vector.tensor_tensor(total[:], all_d[:], all_y[:], ALU.add)

            return total, step

        for c, (c0, width) in enumerate(CHUNKS):
            first, first_step = branch_sums("first", c, n1_t, n3_t, c in FUSED_FIRST, None)
            second, second_step = branch_sums("second", c, n2_t, n4_t, c in FUSED_SECOND, None)
            for t in range(PACK):
                if c == 0:
                    nc.scalar.activation(y[t][:], y_ps[t][:], ACT.Copy, scale=gain_size[:, t : t + 1])
                    if t < D_ON_VECTOR:
                        nc.vector.tensor_scalar(d[t][:], d_ps[t][:], gain_size[:, t : t + 1], None, ALU.mult)
                    else:
                        nc.scalar.activation(d[t][:], d_ps[t][:], ACT.Copy, scale=gain_size[:, t : t + 1])
                first_step(t)
                second_step(t)
            if c == 0:
                w3_grouped = sb.tile([P, PACK * N], BF16, name="w3_grouped", tag="late", align_bytes=64)
                nc.vector.tensor_copy(
                    w3_grouped[:].rearrange("p (c i j) -> p c j i", i=4, j=PACK),
                    w3_raw[:].rearrange("p j (c i) -> p c j i", i=4),
                )
                quantize(w3_q[0], w3_q[1], w3_grouped, 0, N)
                for u in range(PACK):
                    bank = psum.tile([P, S], F32, name="h_ps%d" % u, tag="bank%d" % u)
                    h_ps.append(bank)
            z_size = sb.tile([P, PACK * width], BF16, name="z_size%d" % c, align_bytes=64)
            nc.vector.tensor_tensor(
                z_size[:].rearrange("p (c i t) -> p c t i", i=4, t=PACK),
                first[:].rearrange("p t (c i) -> p c t i", i=4),
                second[:].rearrange("p t (c i) -> p c t i", i=4),
                ALU.max,
            )
            z_grouped = sb.tile([P, PACK * width], BF16, name="z_grouped%d" % c, align_bytes=64)
            nc.vector.tensor_tensor(
                z_grouped[:], z_size[:], signs[:, 0:width, :].rearrange("p s t -> p (s t)"), ALU.mult
            )
            z_q = quantized_tiles("z%d" % c, width)
            quantize(z_q[0], z_q[1], z_grouped, 0, width)
            for u in range(PACK):
                product(h_ps[u][:, c0 : c0 + width], w3_q, u, z_q[0][:], z_q[1][:])
            for u in range(PACK):
                if c == len(CHUNKS) - 1 and u < H_ON_VECTOR:
                    nc.vector.tensor_copy(h[u][:, c0 : c0 + width], h_ps[u][:, c0 : c0 + width])
                else:
                    nc.scalar.copy(h[u][:, c0 : c0 + width], h_ps[u][:, c0 : c0 + width])

        pairs, squares, roots = [], [], []
        for u in range(PACK):
            pair = sb.tile([P, 2 * W], F32, name="pair%d" % u, align_bytes=64)
            nc.scalar.activation(pair[:, 0:W], h[u][:].indirect(n5_t[:]), ACT.Copy, scale=-0.5)
            nc.vector.tensor_copy(pair[:, W : 2 * W], h[u][:].indirect(n6_t[:]))
            pairs.append(pair)
        for u in range(PACK):
            square = sb.tile([P, 2 * W], F32, name="square%d" % u, tag="row_tile%d" % u, align_bytes=64)
            if u % 2 == 0:
                nc.vector.tensor_tensor(square[:], pairs[u][:], pairs[u][:], ALU.mult)
            else:
                nc.scalar.activation(square[:], pairs[u][:], ACT.Square)
            squares.append(square)
        for u in range(PACK):
            radicand = sb.tile([P, W], F32, name="radicand%d" % u, align_bytes=64)
            nc.vector.scalar_tensor_tensor(
                radicand[:], squares[u][:, 0:W], 4.0, squares[u][:, W : 2 * W], ALU.mult, ALU.add
            )
            ra = sb.tile([P, W], F32, name="ra%d" % u, align_bytes=64)
            nc.scalar.activation(ra[:], radicand[:], ACT.Sqrt, bias=0.25)
            roots.append(ra)
        results = [
            sb.tile([P, S], F32, name="result%d" % u, tag="row_tile%d" % (0, 2, 1, 3)[u], align_bytes=64)
            for u in range(PACK)
        ]

        def put_ra(u):
            nc.scalar.activation(results[u][:].indirect(n5_t[:]), roots[u][:], ACT.Copy)

        def put_rb(u):
            nc.vector.tensor_tensor(
                results[u][:].indirect(n6_t[:]), pairs[u][:, W : 2 * W], pairs[u][:, 0:W], ALU.add
            )

        def store(u):
            queue = nc.scalar if u % 2 == 0 else nc.sync
            queue.dma_start(out=out[u * P : (u + 1) * P, :], in_=results[u][:])

        for u in range(0, PACK, 2):
            put_ra(u)
            put_rb(u + 1)
        for u in range(0, PACK, 2):
            put_rb(u)
            store(u)
            put_ra(u + 1)
            store(u + 1)
